import numpy as np, ml_dtypes
CORES = [2,6,10,14,18,22,26,30]
N = 8
BF = ml_dtypes.bfloat16
def gentries(a):
    return np.ascontiguousarray(a.reshape(8, 16, -1).transpose(0, 2, 1)).reshape(8, -1)
def gtable(e):
    e = np.asarray(e); return np.ascontiguousarray(e.reshape(8, -1, 16).transpose(0, 2, 1)).reshape(128, -1).astype(np.int32)
V, E, LB, ST, RO = 4096, 512, 9, 4, 4
def parts(rng):
    Q = 8 * N; q = np.arange(Q)[:, None]; k = np.arange(V)[None, :]
    o = np.argsort(rng.random((Q, V)), axis=1)
    x = np.zeros((Q, V, 16), np.float32); x[q, o] = np.linspace(235.0, 20.0, V)[None, :, None]
    x = x + rng.integers(4, 48, (Q, 1, 1)).astype(np.float32) * rng.standard_normal((Q, V, 16), dtype=np.float32)
    x = np.clip(np.floor(x), 0, 255)
    top = rng.integers(40, 700, (Q, 1)); nx = k + rng.integers(1, top + 1, (Q, V))
    nx = np.where((nx >= V) | (rng.random((Q, V)) < 0.015625), k, nx)
    S = np.zeros((Q, V), np.int64); S[q, o] = o[q, nx]
    pa = rng.integers(0, V, (Q, E)); far = np.where(rng.random((Q, E)) < 0.5, rng.integers(1, V, (Q, E)), rng.integers(1, 301, (Q, E)))
    a = o[q, pa]; b = o[q, (pa + far) % V]
    sa = S[q, a]; b = np.where((rng.random((Q, E)) < 0.0625) & (sa != a), sa, b)
    ix = np.where(rng.random((Q, E)) < 0.0625, rng.integers(0, E, (Q, E)), np.arange(E)[None, :])
    return x, S, a[q, ix], b[q, ix]
def pack(x, S, a, b):
    return {"x": np.ascontiguousarray(np.asarray(x).reshape(N, 8, V, 16).transpose(0, 1, 3, 2)).reshape(N, 128, V).astype(np.float32).astype(BF),
            "succ": np.ascontiguousarray(S.reshape(N, 8, V)).astype(np.int32),
            "ea": np.stack([gtable(e) for e in a.reshape(N, 8, E)]), "eb": np.stack([gtable(e) for e in b.reshape(N, 8, E)])}
def setup_inputs(rng):
    return pack(*parts(rng))
def setup_inputs_ties(rng):
    x, S, a, b = parts(rng); Q = 8 * N
    D = np.zeros((5, 16), np.int64); D[1, :8] = 1; D[1, 8:] = -1; D[2, :9] = 1; D[2, 9:] = -1; D[3, 0] = 1; D[4, 15] = -1
    A = rng.integers(1, 255, (Q, 1, 16)); A[3::8] = rng.choice(np.array([0, 255]), (N, 1, 16))
    y = np.clip(A + D[rng.integers(0, 5, (Q, V))], 0, 255)
    y[5::8] = A[5::8]; y[7::8] = x[7::8].astype(np.int64)
    for i in range(6, Q, 8):
        S[i] = np.where(S[i] % (V - 1) == 0, np.arange(V), S[i]); S[i, 0] = 0; S[i, V - 1] = V - 1
        hit = (a[i] % (V - 1) == 0) | (b[i] % (V - 1) == 0)
        a[i] = np.where(hit, 1, a[i]); b[i] = np.where(hit, 2, b[i])
        j = int(rng.integers(0, E)); a[i, j] = 0; b[i, j] = V - 1
        y[i, 0] = np.minimum(y[i, 0], 200); y[i, V - 1] = y[i, 0]; y[i, V - 1, int(rng.integers(0, 16))] += 50
    return pack(y, S, a, b)
def setup_inputs_crowd(rng):
    x, S, a, b = parts(rng); k = np.arange(E); v = np.arange(V)
    used = np.array(sorted({(ST * n + j) % LB for n in range(RO) for j in range(1, ST)}))
    hub = rng.permutation(V)
    for i in range(8 * N):
        g = i % 8; p = rng.permutation(V)
        if g in (0, 2, 4):
            d = (1, ST + 1, int(rng.choice(used)))[g // 2]; m = k & ~(1 << d)
            a[i] = p[2 * m]; b[i] = p[2 * m + 1]; S[i] = v
        elif g == 1:
            y = rng.permutation(E); j = np.arange(E - 257)
            a[i, y[:257]] = hub[0]; b[i, y[:257]] = hub[1]
            a[i, y[257:]] = hub[2 + 2 * j]; b[i, y[257:]] = hub[3 + 2 * j]
            S[i] = v; x[i] = np.minimum(x[i], 254); x[i, hub[0]] = 255
        elif g == 3:
            a[i] = p[rng.integers(0, 8, E)]; b[i] = p[8 + rng.integers(0, V - 8, E)]; x[i, p[:8]] = 255
        elif g == 5 and i // 8 == N - 1:
            a[i] = p[2 * k]; b[i] = p[2 * k + 1]; S[i] = v
        elif g == 5:
            n = V // 8
            if (i // 8) % 2 == 0: H = int(rng.integers(0, V - n + 1)) + np.arange(n)
            else: H = 8 * np.arange(n) + int(rng.integers(0, 8))
            z = rng.permutation(np.setdiff1d(v, H)); y = rng.permutation(E); j = np.arange(E - n)
            w = np.concatenate([z[:(ST - 1) * n].reshape(ST - 1, n), rng.permutation(H)[None, :]]); z = z[(ST - 1) * n:]
            S[i] = v; S[i, w[:-1]] = w[1:]
            x[i] = rng.integers(0, 128, (V, 16)); x[i, w] += 128
            a[i, y[:n]] = w[0]; b[i, y[:n]] = rng.permutation(z)[:n]
            a[i, y[n:]] = z[2 * j]; b[i, y[n:]] = z[2 * j + 1]
        elif g == 6:
            y = rng.permutation(k[((k >> 1) & 1) == 0]); c = np.concatenate([k[((k >> 1) & 1) == 1], y[:1]]); j = np.arange(E // 2 - 1)
            a[i, c] = hub[0]; b[i, c] = hub[1 + rng.permutation(E // 2 + 1)]
            a[i, y[1:]] = hub[E + 2 * j]; b[i, y[1:]] = hub[E + 2 * j + 1]
            S[i] = v; x[i] = np.minimum(x[i], 254); x[i, hub[0]] = 255
        else:
            m = np.where(((k >> 1) & 1) == 1, k & ~8, k)
            a[i] = p[2 * m]; b[i] = p[2 * m + 1]; S[i] = v
    return pack(x, S, a, b)
def setup_inputs_chains(rng):
    Q = 8 * N; q = np.arange(Q)[:, None]; k = np.arange(V)[None, :]
    C = rng.choice(np.array([2, 3, 4, 8, 16]), (Q, 1)); o = np.argsort(rng.random((Q, V)), axis=1)
    nx = k + C; nx = np.where(nx >= V, k, nx)
    S = np.zeros((Q, V), np.int64); S[q, o] = o[q, nx]
    x = np.zeros((Q, V, 16)); x[q, o] = np.floor(np.linspace(250.0, 1.0, V)[None, :, None] + 0.0625 * np.arange(16)[None, None, :])
    pa = rng.integers(0, V - 32, (Q, E)); pb = pa + rng.integers(1, C, (Q, E)); turn = rng.random((Q, E)) < 0.5
    return pack(x, S, o[q, np.where(turn, pb, pa)], o[q, np.where(turn, pa, pb)])
def setup_inputs_ends(rng):
    x, S, a, b = parts(rng); v = np.arange(V)
    x[0::2] = rng.choice(np.array([0.0, 255.0]), (4 * N, V, 16))
    S[0::8] = rng.integers(0, V, (N, V)); S[1::8] = 0; S[2::8] = V - 1; S[3::8] = V - 1 - v; S[4::8] = (v + 1) % V
    S[5::8] = v ^ 1; b[5::8] = a[5::8] ^ 1
    x[5::16] = rng.integers(0, 64, (N // 2, V, 16)) + 64 * (3 - v % 4)[None, :, None]
    S[5::16] = v - v % 4 + (v + 1) % 4; a[5::16] = 4 * rng.integers(0, V // 4, (N // 2, E)); b[5::16] = a[5::16] + 2
    w = 2 + rng.permutation(V - 4); M = V - 4 - 2 * ST
    for i in range(6, 8 * N, 8):
        S[i] = v; S[i, w[2 * ST:]] = rng.choice(w[2 * ST:], M)
        u = rng.integers(0, M, E); a[i] = w[2 * ST + u]; b[i] = w[2 * ST + (u + rng.integers(1, M, E)) % M]
        for c, (e, low) in enumerate(((0, 1), (V - 1, V - 2))):
            way = np.append(w[c * ST:(c + 1) * ST], e)
            S[i, way[:-1]] = way[1:]; x[i, way] = 255; x[i, low] = 0
        j = rng.permutation(E)[:2]
        a[i, j] = np.array([w[0], V - 2]); b[i, j] = np.array([1, w[ST]])
    a[7::8] = V - 1; b[7::8] = rng.integers(0, V - 1, (N, E))
    return pack(x, S, a, b)
def setup_inputs_spread(rng):
    Q = 8 * N
    x = np.minimum(np.floor(np.exp2(8 * rng.random((Q, V, 1))) * rng.random((Q, V, 16))), 255)
    S = rng.integers(0, V, (Q, V)); S = np.where(rng.random((Q, V)) < 0.0625, np.arange(V)[None, :], S)
    a = rng.integers(0, V, (Q, E)); b = (a + rng.integers(1, V, (Q, E))) % V
    return pack(x, S, a, b)
def check_inputs(d):
    bad = []; v = np.asarray(d["x"]).astype(np.float32)
    if not np.all((v >= 0) & (v <= 255) & (v == np.floor(v))): bad.append("x")
    for k in ("succ", "ea", "eb"):
        if np.min(d[k]) < 0 or np.max(d[k]) > V - 1: bad.append("range of " + k)
    if np.any(np.asarray(d["ea"]) == np.asarray(d["eb"])): bad.append("an edge with equal ends")
    return bad
def above(X, a, b):
    q = np.arange(X.shape[0])[:, None]
    m = np.add.reduce(np.sign(X[q, a] - X[q, b]), axis=2)
    return (m > 0) | ((m == 0) & (a < b))
def reference(x, succ, ea, eb):
    Q = 8 * N; q = np.arange(Q)[:, None]; lane = np.arange(E)[None, :]; qq = np.broadcast_to(q, (Q, E))
    X = np.ascontiguousarray(x.astype(np.float32).astype(np.int32).reshape(Q, 16, V).transpose(0, 2, 1))
    S = np.array(succ, np.int64).reshape(Q, V)
    fa = np.concatenate([gentries(e) for e in ea]).astype(np.int64); fb = np.concatenate([gentries(e) for e in eb]).astype(np.int64)
    a, b = fa, fb
    for rnd in range(RO):
        up = above(X, a, b); h = np.where(up, a, b); l = np.where(up, b, a)
        done = np.zeros((Q, E), bool); out = np.zeros((Q, E), bool)
        for k in range(ST):
            act = ~done & ~out
            s = S[q, h]
            met = act & (s == l)
            walk = act & ~met & (s != h) & above(X, s, l)
            ask = act & ~met & ~walk
            place = q * V + h
            n = np.bincount(place[ask], minlength=Q * V)[place]
            sole = ask & (n == 1); into = sole & (s != h)
            S[qq[sole], h[sole]] = l[sole]
            done = done | met | (sole & (s == h))
            h, l = np.where(into, l, np.where(walk, s, h)), np.where(into, s, l)
            out = ask & (n > 1) & (((lane >> ((rnd * ST + k + 1) % LB)) & 1) == 1)
        X = X + np.clip(X[q, S] - X, -1, 1)
        a = np.roll(np.where(done, fa, h), 8, axis=0); b = np.roll(np.where(done, fb, l), 8, axis=0)
        fa = np.roll(fa, 8, axis=0); fb = np.roll(fb, 8, axis=0)
    return {"ys": S.reshape(N, 8, V).astype(np.float32), "yx": np.ascontiguousarray(X.transpose(0, 2, 1)).reshape(N, 128, V).astype(np.float32).astype(BF)}

from concourse.mybir import AluOpType, ActivationFunctionType

RO, ST_, NL, V_, WP = 4, 4, 512, 4096, 5120
NA, NB, PED = 10, 14, (3,)
_t, _w = ("sbuf", [128, V_], "bfloat16"), ("sbuf", [128, NL], "bfloat16")
_l, _d, _f = ("sbuf", [128, 4, 8], "float32"), ("sbuf", [128, 12, 8], "float32"), ("sbuf", [128, 128], "float32")
_h, _i, _c8 = ("sbuf", [128, 128], "float16"), ("sbuf", [128, 128], "bfloat16"), ("sbuf", [128, 8], "bfloat16")
_b, _bl = ("psum", [128, 512], "float32"), ("psum", [128, 64, 8], "float32")
_r, _rl = ("sbuf", [128, 16, 8], "float16"), ("sbuf", [128, 64], "uint16")
SCRATCH = {
    "xb": _t, "yt": _t, "qt": _t, "pt": ("sbuf", [128, WP], "bfloat16"), "sg": _t, "t2": _t, "asf": _t, "bits": _t, "cf": _t, "dfl": _t,
    "suc": ("sbuf", [128, 256], "int32"), "suf": ("sbuf", [128, 256], "float16"), "sut": ("sbuf", [128, 256], "float16"),
    "sli": ("sbuf", [128, 256], "uint16"), "eai": ("sbuf", [128, 64], "int32"),
    "idf": _f, "m16": _f, "pci": ("sbuf", [128, 1], "int32"), "c8": ("sbuf", [128, 8], "float32"),
    "lh": _f, "lhi": ("sbuf", [128, 128], "int32"), "lhj": ("sbuf", [128, 128], "int32"),
    "low": ("sbuf", [128, 64], "bfloat16"), "hig": ("sbuf", [128, 64], "float32"),
    "ioh": ("sbuf", [128, 64], "bfloat16"), "ihn": ("sbuf", [128, 64], "bfloat16"), "iol": ("sbuf", [128, 64], "bfloat16"),
    "dm": _l, "jt": ("sbuf", [128, 4, 8], "int32"), "bm": ("sbuf", [128, 32, 8], "int32"), "kk": ("sbuf", [128, 4, 8], "float16"),
    "pi": ("sbuf", [128, 8], "int32"), "pf": ("sbuf", [128, 16], "float32"), "mc": ("sbuf", [128, 8], "float32"),
    "i16": _h, "n16": _h, "ib": _i, "nib": _i, "k16": _h, "kb": _i,
    "ex": ("sbuf", [128, 8, 128], "float16"), "tr": ("sbuf", [128, 4, 128], "float16"),
    "sel": ("sbuf", [128, 16, 128], "bfloat16"), "ba": ("sbuf", [128, 16, 128], "bfloat16"),
    "wp": _c8, "wn": _c8, "wh": _c8, "vw": _c8, "gcn": ("sbuf", [128, 3, 8], "bfloat16"), "wy": ("sbuf", [128, 32], "bfloat16"),
    "st": ("sbuf", [128, 12, 8], "float16"), "la": ("sbuf", [128, 96], "uint16"),
    "lor": ("sbuf", [128, 32], "int32"), "lou": ("sbuf", [128, 32], "uint16"), "r": ("sbuf", [128, 12, 64], "float16"),
    "as_": _w, "yl": _w, "bt": _w, "vt": _w, "ql": _w, "tm": _w, "gm": _w, "dl": _w,
    "ohl": ("sbuf", [128, 32, 64], "bfloat16"), "ohv": ("sbuf", [128, 16, 64], "bfloat16"), "ohs": ("sbuf", [128, 16, 64], "bfloat16"),
    "sq": ("sbuf", [128, 16, 64], "bfloat16"), "c2": ("sbuf", [128, 256], "bfloat16"), "dt_": ("sbuf", [128, 256], "bfloat16"),
    "hi": ("sbuf", [128, 4, 8], "int32"), "nh": _l, "lo": _l, "dn": _l, "sgm": _l, "sg1": _l, "sc": _l, "y1": _l, "ask": _l,
    "wk": _l, "wd": _l, "ne": _l, "qq": _l, "nd": _l, "act": _l, "an": _l, "asr": _l, "abm": _l, "ta": _l, "tb": _l,
    "del_": _d, "md": _d, "bs": _d, "tt": _d, "t8": ("sbuf", [128, 8, 8], "float32"),
    "rx0": _r, "rx1": _r, "rx2": _r, "rx3": _r, "rl0": _rl, "rl1": _rl, "rl2": _rl, "rl3": _rl,
    "px0": _r, "px1": _r, "px2": _r, "pl0": _rl, "pl1": _rl, "pl2": _rl,
    "yso": ("sbuf", [128, 1024], "float32"),
    "b0": _b, "bz": _bl, "bd": _bl, "bc": _b, "be": _b, "bn": _bl, "bl": _b, "b7": _b,
}
SEMAPHORES = ["V", "S", "T", "G", "ls", "ar1", "ar2", "ar3"] + ["d%d" % i for i in range(24)]
BANKS = ("b0", "bz", "bd", "bc", "be", "bn", "bl", "b7")


def rank_program(g, core, T, topo):
    rank = T.rank_of(core)
    if rank is None:
        return
    A, F = AluOpType, ActivationFunctionType
    N = len(T.cores)

    queue = {"V": g.vector, "S": g.scalar, "T": g.tensor, "G": g, "Y": g.sync}
    cnt, know, snap, wr, rd = {}, {q: {} for q in queue}, {}, {}, {}
    ndma = [0]

    def sync(q, reads, writes):
        tok = {}

        def want(s, v):
            tok[s] = max(tok.get(s, 0), v)
        for k in reads:
            for s, v in wr.get(k, {}).items():
                if not (k in BANKS and s == q):
                    want(s, v)
            if k in BANKS:
                for s, v in rd.get(k, {}).items():
                    if s != q:
                        want(s, v)
        for k in writes:
            for d in (wr, rd):
                for s, v in d.get(k, {}).items():
                    if s != q:
                        want(s, v)
        kq = know[q]
        todo = {s: v for s, v in tok.items() if kq.get(s, 0) < v}
        for s in list(todo):
            if any(o != s and snap[(o, todo[o])].get(s, 0) >= todo[s] for o in todo if o != s):
                del todo[s]
        for s, v in todo.items():
            queue[q].wait_ge(T.sem[s], v)
        for s, v in todo.items():
            for o, u in snap[(s, v)].items():
                kq[o] = max(kq.get(o, 0), u)
            kq[s] = max(kq.get(s, 0), v)

    def mark(s, v, kq, reads, writes):
        d = dict(kq)
        d[s] = v
        snap[(s, v)] = d
        for k in reads:
            rd.setdefault(k, {})[s] = v
        for k in writes:
            wr.setdefault(k, {})[s] = v

    def op(q, call, reads, writes):
        sync(q, reads, writes)
        call().then_inc(T.sem[q], 1)
        cnt[q] = cnt.get(q, 0) + 1
        mark(q, cnt[q], know[q], reads, writes)

    def dma(q, out, in_, reads, writes):
        sync(q, reads, writes)
        s = "d%d" % ndma[0]
        ndma[0] += 1
        queue[q].dma_start(out, in_).then_inc(T.sem[s], 16)
        cnt[s] = 16
        mark(s, 16, know[q], reads, writes)

    def vts(out, in0, s1, s2, o0, o1, reads, writes):
        if s2 is None:
            op("V", lambda: g.vector.tensor_scalar(out, in0, s1, None, o0), reads, writes)
        else:
            op("V", lambda: g.vector.tensor_scalar(out, in0, s1, s2, o0, o1), reads, writes)

    def vtt(out, a, b, o, reads, writes):
        op("V", lambda: g.vector.tensor_tensor(out, a, b, o), reads, writes)

    def vcp(out, a, reads, writes):
        op("V", lambda: g.vector.tensor_copy(out, a), reads, writes)

    def fill(ap, c, writes):
        op("V", lambda: g.vector.memset(ap, c), [], writes)

    def act(out, a, f, reads, writes, bias=0.0, scale=1.0):
        op("S", lambda: g.scalar.activation(out, a, f, bias=bias, scale=scale), reads, writes)

    def mm(out, l, r, s, e, reads, bank):
        op("T", lambda: g.tensor.matmul(out, l, r, s, e), reads, [bank])

    def io(out, pat, base, cm, key):
        op("G", lambda: g.iota(out, pat, base, cm, allow_small_or_imprecise_dtypes=True), [], [key])

    C8 = list(range(8))
    YK, QK = ["y%d" % c for c in C8], ["q%d" % c for c in C8]
    PK, BK = ["p%d" % c for c in C8], ["bits%d" % c for c in C8]
    CH = [slice(512 * c, 512 * c + 512) for c in C8]
    SGK = ["sgs", "sgv"]
    SLK = ["sli0", "sli1"]
    sl_, l_, h_ = slice(0, 4), slice(4, 8), slice(8, 12)

    dma("Y", T.suc[:], T.succ[:], [], ["suc"])
    dma("Y", T.eai[:, 0:32], T.ea[:], [], ["eai"])
    dma("Y", T.eai[:, 32:64], T.eb[:], [], ["eaj"])
    for c in range(4):
        dma("Y", T.xb[:, c * 1024:c * 1024 + 1024], T.x[:, c * 1024:c * 1024 + 1024], [], ["xd%d" % c])

    io(T.pci[:], [[0, 1]], 0, 1, "pci")
    io(T.c8[:], [[1, 8]], 0, 0, "c8")
    io(T.m16[:], [[0, 8], [1, 16]], 0, 0, "m16")
    io(T.lh[:, 0:64], [[1, 64]], 0, 0, "lh")
    io(T.lh[:, 64:128], [[64, 64]], 0, 0, "lh")
    io(T.idf[:], [[1, 128]], 0, -1, "idf")
    io(T.dm[:], [[256, 4], [0, 8]], 2048, 2, "dm")
    io(T.jt[:], [[128, 4], [0, 8]], 0, 1, "jt")
    io(T.ioh[:], [[64, 64]], -2048, 0, "ioh")
    io(T.ihn[:], [[-64, 64]], 2048, 0, "ihn")
    io(T.iol[:], [[1, 64]], 0, 0, "iol")
    io(T.wy[:], [[0, 32]], 0, 0, "wy0")
    io(T.sel[:], [[0, 16], [0, 128]], 0, 0, "sel0")
    io(T.ba[:], [[0, 16], [0, 128]], 0, 0, "ba0")
    for b in range(4):
        vts(T.pi[:, b:b + 1], T.pci[:], b, 1, A.arith_shift_right, A.bitwise_and, ["pci"], ["pi"])
    vts(T.pi[:, 4:5], T.pci[:], 15, None, A.bitwise_and, None, ["pci"], ["pi"])
    vts(T.pi[:, 5:6], T.pci[:], 4, None, A.arith_shift_right, None, ["pci"], ["pi"])
    for b in range(4):
        vts(T.pf[:, b:b + 1], T.pi[:, b:b + 1], float(2 ** (2 ** b) - 1), 1.0, A.mult, A.add, ["pi"], ["pf"])
    vcp(T.pf[:, 4:6], T.pi[:, 4:6], ["pi"], ["pf"])
    fill(T.tr[:], 0.0, ["tr"])
    vtt(T.pf[:, 6:8], T.pf[:, 0:2], T.pf[:, 2:4], A.mult, ["pf"], ["pg"])
    vts(T.kb[:], T.m16[:], T.pf[:, 4:5], None, A.is_equal, None, ["m16", "pf"], ["kb"])
    vts(T.mc[:], T.c8[:], T.pf[:, 5:6], None, A.is_equal, None, ["c8", "pf"], ["mc"])
    vtt(T.pf[:, 8:9], T.pf[:, 6:7], T.pf[:, 7:8], A.mult, ["pg"], ["pw"])
    vts(T.k16[:], T.m16[:], T.pf[:, 4:5], None, A.is_equal, None, ["m16", "pf"], ["k16"])
    op("V", lambda: g.vector.reciprocal(T.pf[:, 9:10], T.pf[:, 8:9]), ["pw"], ["ipw"])
    vts(T.wp[:], T.mc[:], T.pf[:, 8:9], None, A.mult, None, ["mc", "pw"], ["wp"])
    vts(T.wn[:], T.mc[:], T.pf[:, 8:9], -1.0, A.mult, A.mult, ["mc", "pw"], ["wn"])
    vts(T.lhi[:], T.lh[:], T.pf[:, 9:10], -0.5 + 2.0 ** -13, A.mult, A.add, ["lh", "ipw"], ["lhi"])
    vts(T.wh[:], T.mc[:], T.pf[:, 8:9], 0.5, A.mult, A.mult, ["mc", "pw"], ["wh"])
    vts(T.lhj[:], T.lhi[:], 1, None, A.bitwise_and, None, ["lhi"], ["lhj"])
    vts(T.vw[:], T.mc[:], 4096.0, None, A.mult, None, ["mc"], ["vw"])
    vts(T.low[:], T.lhj[:, 0:64], 2.0, None, A.mult, None, ["lhj"], ["low"])
    vts(T.hig[:], T.lhj[:, 64:128], 2.0, -1.0, A.mult, A.add, ["lhj"], ["hig"])

    def t2_part(a, b):
        for c in range(a, b):
            act(T.t2[:, 128 * c:128 * c + 128], T.kb[:], F.Copy, ["kb"], ["t2"])
    t2_part(0, 8)
    for gb in range(2):
        for cb in range(2):
            for ga in range(4):
                k = 16 * (2 * ga + gb)
                vts(T.tr[:, gb * 2 + cb, k:k + 16], T.k16[:, 0:16], T.mc[:, 2 * ga + cb:2 * ga + cb + 1], None, A.mult, None, ["k16", "mc", "tr"], ["trw"])
    vts(T.suf[:], T.suc[:], -2048.0, None, A.add, None, ["suc"], ["suf"])
    op("V", lambda: g.vector.transpose(T.sut[:], T.suf[:]), ["suf"], ["sut"])
    for c in range(16):
        cl, cb = c // 2, c % 2
        for gb in range(2):
            mm(T.be[:, c:256:16], T.tr[:, gb * 2 + cb, :], T.sut[:, 32 * cl + 16 * gb:32 * cl + 16 * gb + 16], gb == 0, gb == 1, ["trw", "sut"], "be")
    for c in range(64):
        o = T.sg[:, c * 64:c * 64 + 64]
        if c % 2:
            act(o, T.low[:], F.Identity, ["low", "hig"], ["sgs"], bias=T.hig[:, c:c + 1])
        else:
            vts(o, T.low[:], T.hig[:, c:c + 1], None, A.add, None, ["low", "hig"], ["sgv"])
    vts(T.ib[:], T.idf[:], 0.0, None, A.is_equal, None, ["idf"], ["ib"])
    vcp(T.rl0[:, 0:32], T.eai[:, 0:32], ["eai"], ["rl0"])
    vcp(T.rl0[:, 32:64], T.eai[:, 32:64], ["eaj"], ["rl0"])
    for x, buf, key in ((0, T.bt, "bt"), (1, T.gm, "gm")):
        vts(buf[:], T.sg[:].indirect(T.rl0[:, 32 * x:32 * x + 32]), 0.0, None, A.is_gt, None, SGK + ["rl0"], [key])
        for q in range(4):
            mm(T.bz[:, x * 4 + q, :], buf[:, 128 * q:128 * q + 128], T.wp[:], True, True, [key, "wp"], "bz")
    spare = (("b7", T.b7), ("bc", T.bc), ("bl", T.bl))
    for c in C8:
        act(T.yt[:, CH[c]], T.xb[:, CH[c]], F.Identity, ["xd%d" % (c // 2)], [YK[c]], bias=1.0)
        bk, bb = spare[c % 3]
        mm(bb[:], T.ib[:], T.yt[:, CH[c]], True, True, ["ib", YK[c]], bk)
        vtt(T.qt[:, CH[c]], bb[:], T.sg[:, CH[c]], A.mult, [bk] + SGK, [QK[c]])
        if c == 0:
            for hf in range(2):
                vts(T.sli[:, 128 * hf:128 * hf + 128], T.be[:, 128 * hf:128 * hf + 128], 2048.0, None, A.add, None, ["be"], [SLK[hf]])
        if c == 1:
            vts(T.rx0[:, 0:8, :], T.bz[:, 0:8, :], -2048.0, None, A.add, None, ["bz"], ["rx0"])
            vts(T.rx0[:, 8:16, :], T.bz[:, 0:8, :], -2048.0, None, A.add, None, ["bz"], ["rx0"])
        if c == 2:
            vts(T.i16[:], T.idf[:], 0.0, None, A.is_equal, None, ["idf"], ["i16"])
            vts(T.nib[:], T.idf[:], 0.0, -1.0, A.is_equal, A.mult, ["idf"], ["nib"])
            vts(T.n16[:], T.idf[:], 0.0, -1.0, A.is_equal, A.mult, ["idf"], ["n16"])
        if c == 3:
            fill(T.ex[:], 0.0, ["ex0"])
        if c == 4:
            for k in C8:
                vcp(T.ex[:, k, 16 * k:16 * k + 16], T.k16[:, 16 * k:16 * k + 16], ["k16", "ex0"], ["ex"])
            fill(T.kk[:], 2048.0, ["kk"])
    t2_part(8, 32)
    for P in range(4):
        for r in range(4):
            for gp in range(2):
                k = 16 * (2 * P + gp)
                act(T.sel[:, P * 4 + r, k:k + 16], T.kb[:, 0:16], F.Copy, ["kb", "mc", "sel0"], ["sel"], scale=T.mc[:, 4 * gp + r:4 * gp + r + 1])

    def late_constants():
        for x in range(3):
            vcp(T.gcn[:, x, :], T.mc[:], ["mc"], ["gcn"])
        for z in range(8):
            vts(T.bm[:, 4 * z:4 * z + 4, :], T.jt[:], z, 1, A.arith_shift_right, A.bitwise_and, ["jt"], ["bm"])
        vcp(T.bs[:, sl_, :], T.dm[:], ["dm"], ["bs"])

    def later_constants():
        for i in range(16):
            act(T.ba[:, i, i::16], T.wh[:], F.Copy, ["wh", "ba0"], ["ba"])
        act(T.wy[:, 0:8], T.wh[:], F.Copy, ["wh", "wy0"], ["wy"])

    def gather_p(q, cs):
        for c in cs:
            o, i = T.pt[:, CH[c]], T.qt[:].indirect(T.sli[:, 32 * c:32 * c + 32])
            if q == "V":
                vcp(o, i, QK + [SLK[c // 4]], [PK[c]])
            else:
                act(o, i, F.Copy, QK + [SLK[c // 4]], [PK[c]])

    def to_lists(x0, x1, src, skey):
        for c in C8:
            vts(T.r[:, x0 * 4:x1 * 4, 8 * c:8 * c + 8], src, T.mc[:, c:c + 1], None, A.mult, None, [skey, "mc"], ["r"])
        for k in C8:
            mm(T.bl[:, x0 * 32:x1 * 32], T.ex[:, k, :], T.r[:, x0 * 4:x1 * 4, k::8], k == 0, k == 7, ["ex", "r"], "bl")

    def digits():
        H = T.st[:, h_, :]
        vts(T.hi[:], H, -31.5, 1.0 / 64, A.add, A.mult, ["st"], ["hi"])
        vts(T.nh[:], T.hi[:], -64.0, None, A.mult, None, ["hi"], ["nh"])
        vtt(T.lo[:], H, T.nh[:], A.add, ["st", "nh"], ["lo"])

    def square(gg):
        for q in (2, 3):
            act(T.sq[:, gg * 2 + q - 2, :], T.ioh[:], F.Square, ["ioh", "nh"], ["sq%d" % gg], bias=T.nh[:, q, gg:gg + 1])

    def start(n):
        rx, rl, kx, kl = T["rx%d" % n], T["rl%d" % n], "rx%d" % n, "rl%d" % n
        act(T.yl[:], T.yt[:].indirect(rl[:, 32:64]), F.Copy, YK + [kl], ["yl"])
        mm(T.bz[:, 0:4, :], T.i16[:], rx[:, 4:8, :], True, False, ["i16", kx], "bz")
        mm(T.bz[:, 0:4, :], T.n16[:], rx[:, 0:4, :], False, False, ["n16", kx], "bz")
        gather_p("S", (0, 1, 2, 4, 5))
        vtt(T.dl[:], T.yt[:].indirect(rl[:, 0:32]), T.yl[:], A.subtract, YK + [kl, "yl"], ["dl"])
        vts(T.vt[:], T.dl[:], -1.0, 1.0, A.max, A.min, ["dl"], ["vt0", "vt1"])
        for q in range(4):
            mm(T.bz[:, q, :], T.vt[:, 128 * q:128 * q + 128], T.vw[:], False, q == 3, ["vt0", "vw"], "bz")
        vtt(T.tb[:], rx[:, 0:4, :], rx[:, 4:8, :], A.subtract, [kx], ["tb"])
        fill(T.nd[:], 1.0, ["nd"])
        fill(T.act[:], 1.0, ["act"])
        vts(T.ta[:], T.bz[:, 0:4, :], 0.0, None, A.is_gt, None, ["bz"], ["ta"])
        vtt(T.wd[:], T.ta[:], T.tb[:], A.mult, ["ta", "tb"], ["wd"])
        vtt(T.st[:, h_, :], rx[:, 4:8, :], T.wd[:], A.add, [kx, "wd"], ["st"])
        vtt(T.st[:, l_, :], rx[:, 0:4, :], T.wd[:], A.subtract, [kx, "wd"], ["st"])
        to_lists(1, 3, T.st[:, 4:12, :], "st")
        digits()
        gather_p("V", (3,))
        vts(T.la[:, 32:96], T.bl[:, 32:96], 2048.0, None, A.add, None, ["bl"], ["la"])
        gather_p("V", (6, 7))

    def step(n, k):
        last = k == ST_ - 1
        H, L = T.st[:, h_, :], T.st[:, l_, :]
        lh = T.la[:, 64:96]
        P = T.pt[:, 0:V_]
        act(T.yl[:], T.yt[:].indirect(T.la[:, 32:64]), F.Copy, YK + ["la"], ["yl"])
        act(T.tm[:], T.t2[:].indirect(lh), F.Copy, ["t2", "la"], ["tm"])
        hv = (("b0", T.b0), ("b7", T.b7))
        for i, (bk, bb) in enumerate(hv):
            mm(bb[:, 0:256], T.nib[:], T.yl[:, 256 * i:256 * i + 256], True, False, ["nib", "yl"], bk)
        for bk, bb, o in (("bd", T.bd, H), ("bz", T.bz, L)):
            mm(bb[:, 0:4, :], T.i16[:], o, True, False, ["i16", "st"], bk)
            mm(bb[:, 0:4, :], T.i16[:], T.kk[:], False, False, ["i16", "kk"], bk)
        for i, (bk, bb) in enumerate(hv):
            w = slice(256 * i, 256 * i + 256)
            act(T.as_[:, w], P.indirect(T.la[:, 64 + 16 * i:80 + 16 * i]), F.Abs, PK + ["la"], ["as%d" % i])
            mm(bb[:, 0:256], T.ib[:], T.as_[:, w], False, True, ["ib", "as%d" % i], bk)
        vts(T.bt[:], P.indirect(lh), 0.0, None, A.is_gt, None, PK + ["la"], ["bt"])
        square(0)
        for i, (bk, bb) in enumerate(hv):
            act(T.vt[:, 256 * i:256 * i + 256], bb[:, 0:256], F.Sign, [bk], ["vt%d" % i])
        for gg in range(1, 8):
            square(gg)
        for q in range(4):
            mm(T.bd[:, q, :], T.bt[:, 128 * q:128 * q + 128], T.wn[:], False, q == 3, ["bt", "wn"], "bd")
        for q in range(4):
            mm(T.bz[:, q, :], T.bt[:, 128 * q:128 * q + 128], T.wn[:], False, False, ["bt", "wn"], "bz")
        for q in range(4):
            mm(T.bz[:, q, :], T.vt[:, 128 * q:128 * q + 128], T.vw[:], False, q == 3, ["vt%d" % (q // 2), "vw"], "bz")
        vts(T.lor[:], T.bl[:, 64:96], 2048.0 - 7.5, 1.0 / 16, A.add, A.mult, ["bl"], ["lor"])

        def low_hot(i):
            gg, q = i // 4, i % 4
            vts(T.ohl[:, i, :], T.iol[:], T.lo[:, q, gg:gg + 1], None, A.is_equal, None, ["iol", "lo"], ["ohl%d" % gg])
        for i in range(NA):
            low_hot(i)
        D, Z = T.bd[:, 0:4, :], T.bz[:, 0:4, :]
        vts(T.dn[:], D, 0.0, None, A.not_equal, None, ["bd"], ["dn"])
        vcp(T.lou[:], T.lor[:], ["lor"], ["lou"])
        vts(T.sg1[:], T.dn[:], 2.0, -1.0, A.mult, A.add, ["dn"], ["sg1"])
        vtt(T.sc[:], H, D, A.subtract, ["st", "bd"], ["sc"])
        vtt(T.sgm[:], T.sg1[:], T.act[:], A.mult, ["sg1", "act"], ["sgm"])
        for i in range(NA, NB):
            low_hot(i)
        vtt(T.y1[:], Z, T.sgm[:], A.mult, ["bz", "sgm"], ["y1"])
        vts(T.ask[:], T.y1[:], 0.0, None, A.is_lt, None, ["y1"], ["ask"])
        cb = (("bc", T.bc), ("b7", T.b7))

        def spread(P4):
            bk, bb = cb[P4 % 2]
            act(T.c2[:, 64 * P4:64 * P4 + 64], bb[:, 64 * P4:64 * P4 + 64], F.Copy, [bk], ["c2%d" % P4])
            for r in range(4):
                mm(T.be[:, r:256:4], T.sel[:, P4 * 4 + r, :], T.c2[:, 64 * P4:64 * P4 + 64], P4 == 0 and r == 0, P4 == 3 and r == 3, ["sel", "c2%d" % P4], "be")
        for P4 in range(4):
            bk, bb = cb[P4 % 2]
            for gg in (2 * P4, 2 * P4 + 1):
                for q in range(4):
                    if gg * 4 + q >= NB:
                        low_hot(gg * 4 + q)
                    if q < 2:
                        vts(T.ohv[:, gg * 2 + q, :], T.ihn[:], T.nh[:, q, gg:gg + 1], T.ask[:, q, gg:gg + 1], A.is_equal, A.mult, ["ihn", "nh", "ask"], ["ohv%d" % gg])
                    else:
                        act(T.ohs[:, gg * 2 + q - 2, :], T.sq[:, gg * 2 + q - 2, :], F.Relu, ["sq%d" % gg, "ask"], ["ohs%d" % gg], bias=T.ask[:, q, gg:gg + 1], scale=-1.0)
                for q in range(4):
                    ob, kb = (T.ohv, "ohv%d" % gg) if q < 2 else (T.ohs, "ohs%d" % gg)
                    p0 = 64 * (gg % 2)
                    mm(bb[p0:p0 + 64, 64 * P4:64 * P4 + 64], T.ohl[:, gg * 4 + q, :], ob[:, gg * 2 + q % 2, :], q == 0, q == 3, ["ohl%d" % gg, kb], bk)
            if P4:
                spread(P4 - 1)
        spread(3)
        act(T.dt_[:], T.be[:, 0:256], F.Relu, ["be"], ["dt"], bias=2.0, scale=-1.0)
        act(T.ql[:], T.qt[:].indirect(T.la[:, 32:64]), F.Copy, QK + ["la"], ["ql"])
        vts(T.wk[:], T.y1[:], 0.0, None, A.is_gt, None, ["y1"], ["wk"])
        vts(T.ne[:], T.y1[:], 0.0, None, A.not_equal, None, ["y1"], ["ne"])
        vtt(T.an[:], T.ask[:], T.dn[:], A.mult, ["ask", "dn"], ["an"])
        vtt(T.wd[:], D, T.wk[:], A.mult, ["bd", "wk"], ["wd"])
        vtt(T.qq[:], T.nd[:], T.act[:], A.subtract, ["nd", "act"], ["qq"])
        vtt(T.del_[:, sl_, :], H, T.dm[:], A.subtract, ["st", "dm"], ["del"])
        vtt(T.del_[:, l_, :], T.sc[:], L, A.subtract, ["sc", "st"], ["del"])
        vtt(T.del_[:, h_, :], L, H, A.subtract, ["st"], ["del"])
        vtt(T.asr[:], T.ask[:], T.an[:], A.subtract, ["ask", "an"], ["asr"])
        vcp(T.bs[:, l_, :], L, ["st"], ["bs"])
        vtt(T.bs[:, h_, :], H, T.wd[:], A.subtract, ["st", "wd"], ["bs"])
        vtt(T.qq[:], T.qq[:], T.ne[:], A.add, ["qq", "ne"], ["qq"])
        vtt(T.md[:, sl_, :], T.del_[:, sl_, :], T.ask[:], A.mult, ["del", "ask"], ["md"])
        vtt(T.md[:, l_, :], T.del_[:, l_, :], T.an[:], A.mult, ["del", "an"], ["md"])
        vtt(T.md[:, h_, :], T.del_[:, h_, :], T.an[:], A.mult, ["del", "an"], ["md"])
        if not last:
            z = (ST_ * n + k + 1) % 9
            vtt(T.abm[:], T.ask[:], T.bm[:, 4 * z:4 * z + 4, :], A.mult, ["ask", "bm"], ["abm"])
        vtt(T.gm[:], T.dt_[:].indirect(T.lou[:]), T.tm[:], A.mult, ["dt", "lou", "tm"], ["gm"])
        for q in range(4):
            mm(T.bn[:, q:12:4, :], T.gm[:, 128 * q:128 * q + 128], T.gcn[:], True, True, ["gm", "gcn"], "bn")
        E1 = T.bn[:, 0:4, :]
        vtt(T.tt[:], T.bn[:, 0:12, :], T.md[:], A.mult, ["bn", "md"], ["tt"])
        vtt(T.st[:], T.bs[:], T.tt[:], A.add, ["bs", "tt"], ["st"])
        if last:
            to_lists(0, 1, T.st[:, sl_, :], "st")
        else:
            to_lists(0, 3, T.st[:], "st")
        vtt(T.ta[:], E1, T.asr[:], A.mult, ["bn", "asr"], ["ta"])
        if not last:
            vtt(T.tb[:], E1, T.abm[:], A.mult, ["bn", "abm"], ["tb"])
            digits()
        vtt(T.nd[:], T.qq[:], T.ta[:], A.subtract, ["qq", "ta"], ["nd"])
        if not last:
            vtt(T.tb[:], T.abm[:], T.tb[:], A.subtract, ["abm", "tb"], ["tb"])
            vtt(T.act[:], T.nd[:], T.tb[:], A.subtract, ["nd", "tb"], ["act"])
        w = 32 if last else 96
        vts(T.la[:, 0:w], T.bl[:, 0:w], 2048.0, None, A.add, None, ["bl"], ["la"])
        op("V", lambda: g.vector.tensor_copy(T.pt[:].indirect(T.la[:, 0:32]), T.ql[:]), ["la", "ql"], PK)

    def send(n):
        rx, px, pl, kp, kq = T["rx%d" % n], T["px%d" % n], T["pl%d" % n], "px%d" % n, "pl%d" % n
        kx = "rx%d" % n
        vtt(T.t8[:, 0:4, :], T.st[:, h_, :], rx[:, 8:12, :], A.subtract, ["st", kx], ["t8"])
        vtt(T.t8[:, 4:8, :], T.st[:, l_, :], rx[:, 12:16, :], A.subtract, ["st", kx], ["t8"])
        vcp(px[:, 8:16, :], rx[:, 8:16, :], [kx], [kp + "f"])
        vtt(T.tt[:, 0:4, :], T.t8[:, 0:4, :], T.nd[:], A.mult, ["t8", "nd"], ["tt"])
        vtt(T.tt[:, 4:8, :], T.t8[:, 4:8, :], T.nd[:], A.mult, ["t8", "nd"], ["tt"])
        vtt(px[:, 0:8, :], rx[:, 8:16, :], T.tt[:, 0:8, :], A.add, [kx, "tt"], [kp])
        to_lists(0, 2, px[:, 0:8, :], kp)

    def send_off(n):
        px, pl, kp, kq = T["px%d" % n], T["pl%d" % n], "px%d" % n, "pl%d" % n
        vts(pl[:], T.bl[:, 0:64], 2048.0, None, A.add, None, ["bl"], [kq])
        dst = T.cores[(rank + 1) % N]
        rid, pid, _ = topo.addr(dst)
        eng = topo.engines(core, dst)[:4]
        m = sum(1 << e for e in eng)
        s = "ar%d" % (n + 1)
        sync("G", [kp, kp + "f", kq], [])
        for o, i in (("rx%d" % (n + 1), px), ("rl%d" % (n + 1), pl)):
            g.remote_dma(T[o][:], i[:], T.sem[s], T.sem["ls"], pid, rid, m)
        nin = len(topo.engines(T.cores[(rank - 1) % N], core)[:4])
        cnt["ls"] = cnt.get("ls", 0) + 2 * len(eng)
        cnt[s] = 2 * nin
        mark(s, cnt[s], {}, [], ["rx%d" % (n + 1), "rl%d" % (n + 1)])

    def finish(n):
        final = n == RO - 1
        ped = () if final else PED

        def table(hf, a, b):
            for i in range(a, b):
                mm(T.be[:, 128 * hf:128 * hf + 128], T.ba[:, i, :], T.bits[:, 2048 * hf + i:2048 * hf + 2048:16], i == 0, i == 15, BK[4 * hf:4 * hf + 4] + ["ba"], "be")
            if b == 16:
                vts(T.sli[:, 128 * hf:128 * hf + 128], T.be[:, 128 * hf:128 * hf + 128], 30720.0 + 2047.5, None, A.add, None, ["be"], [SLK[hf]])

        def names(c):
            bk, bb = (("be", T.be), ("b0", T.b0))[c % 2]
            a = c // 2
            mm(bb[32 * a:32 * a + 32, :], T.wy[:], T.bits[:, CH[c]], True, True, ["wy", BK[c]], bk)

        def begin(c):
            act(T.asf[:, CH[c]], T.pt[:, CH[c]], F.Abs, PK, ["asf%d" % c])
            act(T.bits[:, CH[c]], T.pt[:, CH[c]], F.Sign, PK, [BK[c]])

        def middle(c):
            if c in ped:
                mm(T.b0[:], T.nib[:], T.yt[:, CH[c]], True, False, ["nib", YK[c]], "b0")
                mm(T.b0[:], T.ib[:], T.asf[:, CH[c]], False, True, ["ib", "asf%d" % c], "b0")
                act(T.cf[:, CH[c]], T.b0[:], F.Sign, ["b0"], ["cf%d" % c])
            else:
                vtt(T.dfl[:, CH[c]], T.asf[:, CH[c]], T.yt[:, CH[c]], A.subtract, ["asf%d" % c, YK[c]], ["df%d" % c])
                vts(T.cf[:, CH[c]], T.dfl[:, CH[c]], -1.0, 1.0, A.max, A.min, ["df%d" % c], ["cf%d" % c])
            bk, bb = spare[c % 3]
            mm(bb[:], T.ib[:], T.yt[:, CH[c]], True, False, ["ib", YK[c]], bk)
            mm(bb[:], T.ib[:], T.cf[:, CH[c]], False, True, ["ib", "cf%d" % c], bk)

        def end(c):
            bk, bb = spare[c % 3]
            if not final:
                vtt(T.qt[:, CH[c]], bb[:], T.sg[:, CH[c]], A.mult, [bk] + SGK, [QK[c]])
                act(T.yt[:, CH[c]], bb[:], F.Copy, [bk], [YK[c]])
            else:
                act(T.xb[:, CH[c]], bb[:], F.Copy, [bk], ["xo%d" % c], bias=-1.0)
                dma("Y", T.yx[:, CH[c]], T.xb[:, CH[c]], ["xo%d" % c], [])
        begin(0)
        begin(1)
        if not final:
            send(n)
            send_off(n)
        for c in C8:
            if c + 2 < 8:
                begin(c + 2)
            middle(c)
            if c:
                end(c - 1)
            if final:
                names(c)
            elif c in (3, 4):
                table(0, 8 * (c - 3), 8 * (c - 3) + 8)
            elif c in (5, 6):
                table(1, 8 * (c - 5), 8 * (c - 5) + 8)
        end(7)
        if final:
            for b, (bk, bb) in enumerate((("be", T.be), ("b0", T.b0))):
                vts(T.yso[:, 512 * b:512 * b + 512], bb[:], 30720.0 + 2047.5, None, A.add, None, [bk], ["yso"])
            for a in range(4):
                dma("Y", T.ys[:, 1024 * a:1024 * a + 1024], T.yso[32 * a:32 * a + 8, :], ["yso"], [])

    for n in range(RO):
        start(n)
        if n == 0:
            late_constants()
        for k in range(ST_):
            step(n, k)
            if n == 0 and k == 0:
                later_constants()
        finish(n)

    for s, v in cnt.items():
        g.wait_ge(T.sem[s], v)
